import numpy as np
import ml_dtypes


def mxq(x, axis, fmt="e4m3"):
    dtype, down = {"e4m3": (ml_dtypes.float8_e4m3fn, 7), "e5m2": (ml_dtypes.float8_e5m2, 14)}[fmt]
    v = np.moveaxis(np.asarray(x, np.float32).astype(ml_dtypes.bfloat16).astype(np.float64), axis, -1)
    blocks = v.reshape(v.shape[:-1] + (-1, 32))
    amax = np.abs(blocks).max(-1, keepdims=True)
    byte = np.maximum(np.where(amax > 0, np.frexp(amax)[1] - 1 + 127, 0) - down, 1)
    scale = np.exp2(byte - 127.0)
    codes = (blocks / scale).astype(np.float32).astype(dtype).astype(np.float64)
    return np.moveaxis((codes * scale).reshape(v.shape), -1, axis)


WIDE = False


def mx_kscale(k):
    if not WIDE:
        return np.ones(k)
    levels = np.array([10, -10, 5, -5, 0])
    if k % 512:
        return np.exp2(np.random.permutation(np.resize(levels, k // 32))).repeat(32)
    a = np.empty((k // 512, 16))
    for p in range(k // 512):
        a[p, :8] = np.random.permutation(np.resize(levels, 8))
        for g in range(8):
            far = levels[np.abs(levels - a[p, g]) >= 10]
            a[p, g + 8] = far[np.random.randint(len(far))]
    return np.exp2(a.ravel()).repeat(32)


def f64(x):
    return np.asarray(x).astype(np.float64)


def striped(idx):
    return np.tile(idx.reshape(-1, 16).T, (8, 1)).astype(np.uint16)


def unstriped(offs):
    return offs[:16].T.reshape(-1).astype(np.int64)


def pack_weight(w):
    k, n = w.shape
    w = f64(np.asarray(w, np.float32).astype(ml_dtypes.bfloat16)).reshape(k // 32, 32, n)
    amax = np.abs(w).max(1)
    byte = np.clip(np.where(amax > 0, np.frexp(amax)[1] - 1 + 127 - 7, 1), 1, 254)
    scaled = (w * np.exp2(127.0 - byte)[:, None, :]).reshape(k, n).astype(np.float32)
    words = np.ascontiguousarray(scaled.reshape(k // 512, 128, 4, n).transpose(0, 1, 3, 2)).astype(ml_dtypes.float8_e4m3fn).view(np.uint8)
    return words, np.ascontiguousarray(byte.astype(np.uint8).reshape(k // 512, 16, n))


def unpack_weight(words, scales):
    g, p, n, _ = words.shape
    vals = np.ascontiguousarray(words).view(ml_dtypes.float8_e4m3fn).astype(np.float64) * np.repeat(np.exp2(scales.astype(np.float64) - 127.0), 8, axis=1)[..., None]
    return vals.transpose(0, 1, 3, 2).reshape(g * 512, n)


K, T, S, D, R, G = 512, 2048, 512, 32, 256, 8
P = 2 ** 7


def setup_inputs():
    n = np.random.standard_normal
    s = mx_kscale(K)[:, None]
    perm = (np.random.permutation(D)[:, None] + D * np.arange(G)[None, :]).reshape(-1)
    packed_xT = pack_weight(n((K, T)) * s)
    return {
        "x_words": packed_xT[0],
        "x_scales": packed_xT[1],
        "fm": (n((K, R)) / np.sqrt(K) / s).astype(np.float32),
        "meas": (n((S, R))).astype(np.float32),
        "prec": (np.tile(np.random.uniform(0.05, 0.2, R), (P, 1))).astype(np.float32),
        "prior": (np.tile(0.5 * n(G), (P, 1))).astype(np.float32),
        "gain": (np.tile(np.random.uniform(0.2, 0.8, R), (P, 1))).astype(np.float32),
        "offs": striped(np.random.permutation(T)[:S]),
        "byf": striped(perm),
    }


def reference(x_words, x_scales, fm, meas, prec, prior, gain, offs, byf):
    xq = unpack_weight(x_words, x_scales)[:, unstriped(offs)]
    fmq = mxq(f64(fm), 0, "e4m3")
    y = xq.T @ fmq
    dd = f64(meas) - y
    d2 = ((dd) ** 2) * f64(prec)[:1]
    lm = f64(prior)[:1] - (0.5 * (d2.reshape(len(d2), -1, D).sum(axis=2)))
    ex = np.exp(lm - lm.max(axis=1, keepdims=True))
    mu = ex / ex.sum(axis=1, keepdims=True)
    ww = np.repeat(mu, D, axis=1) * (y + dd * f64(gain)[:1])
    wf = ww[:, unstriped(byf)]
    fu = wf.reshape(len(wf), -1, 8).sum(axis=2)
    return np.tanh(fu)

@@ -1,0 +1,165 @@
+import math
+from contextlib import ExitStack
+
+import concourse.mybir as mybir
+
+K, T, S, D, R, G = 512, 2048, 512, 32, 256, 8
+FLOPS = 2 * K * S * R
+
+F32 = mybir.dt.float32
+BF16 = mybir.dt.bfloat16
+I32 = mybir.dt.int32
+U32 = mybir.dt.uint32
+U16 = mybir.dt.uint16
+U8 = mybir.dt.uint8
+FP8X4 = mybir.dt.float8_e4m3fn_x4
+ALU = mybir.AluOpType
+ACT = mybir.ActivationFunctionType
+AX = mybir.AxisListType
+
+P = 128
+PACK = 4
+TILES = S // P
+ROW = D + 4
+HALF = R // 2
+
+
+def tile_picked_yimm_tanh_p_kernel(
+    tc, x_words, x_scales, fm, meas, prec, prior, gain, offs, byf, out
+):
+    nc = tc.nc
+    with ExitStack() as ctx:
+        keep = ctx.enter_context(tc.tile_pool(name="keep", bufs=1))
+        psum = ctx.enter_context(tc.psum_pool(name="psum", bufs=1))
+
+        def tiles(name, shape, dtype, pool=keep, **kw):
+            return [pool.tile(shape, dtype, name=f"{name}{i}", **kw) for i in range(TILES)]
+
+        offs_sb = keep.tile([P, S // 16], U16)
+        byf_sb = keep.tile([P, R // 16], U16)
+        words_sb = keep.tile([P, T], U32)
+        scales_sb = keep.tile([P, T], U8)
+        fm_raw = keep.tile([P, PACK, R], F32)
+        prec_sb = keep.tile([P, R], F32)
+        gain_sb = keep.tile([P, R], F32)
+        prior_sb = keep.tile([P, G], F32)
+        meas_sb = tiles("meas", [P, R], F32)
+
+        nc.vector.memset(scales_sb[:].bitcast(I32), 0)
+        nc.sync.dma_start(offs_sb[:], offs)
+        nc.sync.dma_start(fm_raw[:], fm.rearrange("(p j) e -> p j e", j=PACK))
+        for q in range(4):
+            nc.sync.dma_start(
+                scales_sb[32 * q : 32 * q + 4, :].bitcast(I32),
+                x_scales[0, 4 * q : 4 * q + 4, :].bitcast(I32),
+            )
+        nc.sync.dma_start(
+            words_sb[:].bitcast(I32), x_words[0].rearrange("p c r -> p (c r)").bitcast(I32)
+        )
+        nc.sync.dma_start(meas_sb[0][:], meas[0:P, :])
+        nc.sync.dma_start(prior_sb[:], prior)
+        nc.sync.dma_start(prec_sb[:], prec)
+        nc.sync.dma_start(gain_sb[:], gain)
+        nc.sync.dma_start(meas_sb[1][:], meas[P : 2 * P, :])
+        nc.sync.dma_start(byf_sb[:], byf)
+        for i in range(2, TILES):
+            nc.sync.dma_start(meas_sb[i][:], meas[i * P : (i + 1) * P, :])
+
+        fm_bf = keep.tile([P, R, PACK], BF16, align_bytes=64)
+        fm_codes = keep.tile([P, R], U32, align_bytes=64)
+        fm_scales = keep.tile([P, R], U8, align_bytes=64)
+        nc.scalar.activation(
+            fm_bf[:].rearrange("p (c i) j -> p c j i", i=4),
+            fm_raw[:].rearrange("p j (c i) -> p c j i", i=4),
+            ACT.Copy,
+        )
+        x_sc = keep.tile([P, S], U8, align_bytes=64)
+        nc.vector.tensor_copy(x_sc[:], scales_sb[:].indirect(offs_sb[:]))
+        nc.vector.quantize_mx(
+            out=fm_codes[:].bitcast(FP8X4),
+            scales=fm_scales[:],
+            in_=fm_bf[:].rearrange("p e j -> p (e j)"),
+        )
+
+        x_codes = tiles("x_codes", [P, P], U32, align_bytes=64)
+        y = tiles("y", [P, R], F32, pool=psum)
+        dd = tiles("dd", [P, R], F32)
+        sq = tiles("sq", [P, R], F32)
+        fit = tiles("fit", [P, G, ROW], F32)
+        step = tiles("step", [P, R], F32)
+        z = tiles("z", [P, R], F32)
+        ww = tiles("ww", [P, R], F32)
+        wf = tiles("wf", [P, R], F32)
+        h = tiles("h", [P, G], F32)
+        low = tiles("low", [P, 1], F32)
+        ex = tiles("ex", [P, G], F32)
+        total = tiles("total", [P, 1], F32)
+        inv = tiles("inv", [P, 1], F32)
+        fu = tiles("fu", [P, D], F32)
+        res = tiles("res", [P, D], F32)
+
+        for i in range(TILES):
+            nc.scalar.activation(fit[i][:, :, D], prior_sb[:], ACT.Copy, scale=-1.0)
+
+        def product(i):
+            cols = P // 16
+            nc.vector.tensor_copy(
+                x_codes[i][:], words_sb[:].indirect(offs_sb[:, i * cols : (i + 1) * cols])
+            )
+            nc.tensor.matmul_mx(
+                out=y[i][:],
+                lhsT=x_codes[i][:].bitcast(FP8X4),
+                lhsT_scale=x_sc[:, i * P : (i + 1) * P],
+                rhs=fm_codes[:].bitcast(FP8X4),
+                rhs_scale=fm_scales[:],
+                start=True,
+                stop=True,
+            )
+
+        def residual(i):
+            nc.vector.tensor_tensor(dd[i][:], meas_sb[i][:], y[i][:], ALU.subtract)
+            nc.scalar.activation(sq[i][:], dd[i][:], ACT.Square, scale=math.sqrt(0.5))
+            nc.vector.tensor_tensor(step[i][:], dd[i][:], gain_sb[:], ALU.mult)
+
+        def weights(i):
+            nc.vector.tensor_tensor(
+                fit[i][:, :, 0:D],
+                sq[i][:].rearrange("p (g d) -> p g d", d=D),
+                prec_sb[:].rearrange("p (g d) -> p g d", d=D),
+                ALU.mult,
+            )
+            nc.vector.tensor_reduce(h[i][:], fit[i][:, :, 0 : D + 1], AX.X, ALU.add)
+            nc.vector.tensor_reduce(low[i][:], h[i][:], AX.X, ALU.min)
+            nc.scalar.activation(
+                ex[i][:], h[i][:], ACT.Exp, bias=low[i][:], scale=-1.0, accum_out=total[i][:]
+            )
+            nc.vector.tensor_tensor(z[i][:], step[i][:], y[i][:], ALU.add)
+
+        def fuse(i):
+            nc.vector.tensor_tensor(
+                ww[i][:].rearrange("p (g d) -> p g d", d=D),
+                z[i][:].rearrange("p (g d) -> p g d", d=D),
+                ex[i][:].unsqueeze(2).to_broadcast([P, G, D]),
+                ALU.mult,
+            )
+            nc.vector.reciprocal(inv[i][:], total[i][:])
+            for u in range(2):
+                cols = HALF // 16
+                nc.scalar.activation(
+                    wf[i][:, u * HALF : (u + 1) * HALF],
+                    ww[i][:].indirect(byf_sb[:, u * cols : (u + 1) * cols]),
+                    ACT.Copy,
+                )
+
+        def finish(i):
+            nc.vector.tensor_reduce(
+                fu[i][:], wf[i][:].rearrange("p (v g) -> p v g", g=G), AX.X, ALU.add
+            )
+            nc.scalar.activation(res[i][:], fu[i][:], ACT.Tanh, scale=inv[i][:])
+            nc.sync.dma_start(out[i * P : (i + 1) * P, :], res[i][:])
+
+        stages = [product, residual, weights, fuse, finish]
+        for turn in range(TILES + len(stages) - 1):
+            for depth, stage in reversed(list(enumerate(stages))):
+                if 0 <= turn - depth < TILES:
+                    stage(turn - depth)

@@ -2,6 +2,7 @@ import math
 from contextlib import ExitStack
 
 import concourse.mybir as mybir
+from concourse.masks import make_identity
 
 K, T, S, D, R, G = 512, 2048, 512, 32, 256, 8
 FLOPS = 2 * K * S * R
@@ -41,11 +42,15 @@ def tile_picked_yimm_tanh_p_kernel(
         scales_sb = keep.tile([P, T], U8)
         fm_raw = keep.tile([P, PACK, R], F32)
         prec_sb = keep.tile([P, R], F32)
-        gain_sb = keep.tile([P, R], F32)
+        gain_col = keep.tile([P, 2], F32)
+        pull = keep.tile([P, 2], F32)
+        ident = keep.tile([P, P], F32)
         prior_sb = keep.tile([P, G], F32)
-        meas_sb = tiles("meas", [P, R], F32)
+        meas_all = keep.tile([P, TILES, R], F32)
+        meas_sb = [meas_all[:, i, :] for i in range(TILES)]
+        meas_rows = meas.rearrange("(i p) e -> p i e", p=P)
 
-        nc.vector.memset(scales_sb[:].bitcast(I32), 0)
+        nc.gpsimd.memset(scales_sb[:].bitcast(I32), 0)
         nc.sync.dma_start(offs_sb[:], offs)
         nc.sync.dma_start(fm_raw[:], fm.rearrange("(p j) e -> p j e", j=PACK))
         for q in range(4):
@@ -56,15 +61,14 @@ def tile_picked_yimm_tanh_p_kernel(
         nc.sync.dma_start(
             words_sb[:].bitcast(I32), x_words[0].rearrange("p c r -> p (c r)").bitcast(I32)
         )
-        nc.sync.dma_start(meas_sb[0][:], meas[0:P, :])
-        nc.sync.dma_start(prior_sb[:], prior)
+        nc.sync.dma_start(meas_all[:], meas_rows)
         nc.sync.dma_start(prec_sb[:], prec)
-        nc.sync.dma_start(gain_sb[:], gain)
-        nc.sync.dma_start(meas_sb[1][:], meas[P : 2 * P, :])
+        nc.sync.dma_start(prior_sb[:], prior)
+        with nc.allow_non_contiguous_dma(reason="one gain value to a partition"):
+            nc.sync.dma_start(gain_col[:], gain[0:1, :].rearrange("o (j p) -> p (o j)", p=P))
         nc.sync.dma_start(byf_sb[:], byf)
-        for i in range(2, TILES):
-            nc.sync.dma_start(meas_sb[i][:], meas[i * P : (i + 1) * P, :])
 
+        make_identity(nc, ident[:])
         fm_bf = keep.tile([P, R, PACK], BF16, align_bytes=64)
         fm_codes = keep.tile([P, R], U32, align_bytes=64)
         fm_scales = keep.tile([P, R], U8, align_bytes=64)
@@ -82,24 +86,31 @@ def tile_picked_yimm_tanh_p_kernel(
         )
 
         x_codes = tiles("x_codes", [P, P], U32, align_bytes=64)
-        y = tiles("y", [P, R], F32, pool=psum)
+        y = [psum.tile([P, R], F32, name=f"y{i}", tag=f"bank{i}") for i in range(TILES)]
         dd = tiles("dd", [P, R], F32)
         sq = tiles("sq", [P, R], F32)
         fit = tiles("fit", [P, G, ROW], F32)
-        step = tiles("step", [P, R], F32)
+        dd_t = tiles("dd_t", [P, 2, P], F32, pool=psum)
+        step_t = tiles("step_t", [P, 2, P], F32)
         z = tiles("z", [P, R], F32)
-        ww = tiles("ww", [P, R], F32)
-        wf = tiles("wf", [P, R], F32)
-        h = tiles("h", [P, G], F32)
+        last = TILES - 1
+        ww = [keep.tile([P, R + 2 * G if i < last else R], F32, name=f"ww{i}") for i in range(TILES)]
+        wf = keep.tile([P, last, R], F32)
+        wf_last = keep.tile([P, R], F32)
+        stats_last = keep.tile([P, last * D], F32, tag="stats_then_fu")
+        h = [ww[i][:, R : R + G] for i in range(last)] + [stats_last[:, 0:G]]
         low = tiles("low", [P, 1], F32)
-        ex = tiles("ex", [P, G], F32)
-        total = tiles("total", [P, 1], F32)
-        inv = tiles("inv", [P, 1], F32)
-        fu = tiles("fu", [P, D], F32)
-        res = tiles("res", [P, D], F32)
+        ex = [ww[i][:, R + G : R + 2 * G] for i in range(last)] + [stats_last[:, G : 2 * G]]
+        total = keep.tile([P, TILES], F32)
+        inv = keep.tile([P, TILES], F32)
+        fu_last = keep.tile([P, D], F32)
+        res = keep.tile([P, last, D], F32)
+        res_last = keep.tile([P, D], F32)
+        out_rows = out.rearrange("(i p) v -> p i v", p=P)
 
         for i in range(TILES):
             nc.scalar.activation(fit[i][:, :, D], prior_sb[:], ACT.Copy, scale=-1.0)
+        nc.scalar.activation(pull[:], gain_col[:], ACT.Copy, bias=-1.0)
 
         def product(i):
             cols = P // 16
@@ -116,50 +127,87 @@ def tile_picked_yimm_tanh_p_kernel(
                 stop=True,
             )
 
+        def grouped(tile):
+            return tile[:].rearrange("p (g d) -> p g d", d=D)
+
         def residual(i):
-            nc.vector.tensor_tensor(dd[i][:], meas_sb[i][:], y[i][:], ALU.subtract)
+            nc.vector.tensor_tensor(dd[i][:], meas_sb[i], y[i][:], ALU.subtract)
             nc.scalar.activation(sq[i][:], dd[i][:], ACT.Square, scale=math.sqrt(0.5))
-            nc.vector.tensor_tensor(step[i][:], dd[i][:], gain_sb[:], ALU.mult)
+
+        def misfit(i):
+            weng = nc.gpsimd if i in (1, 2, 3) else nc.vector
+            weng.tensor_tensor(fit[i][:, :, 0:D], grouped(sq[i]), grouped(prec_sb), ALU.mult)
 
         def weights(i):
-            nc.vector.tensor_tensor(
-                fit[i][:, :, 0:D],
-                sq[i][:].rearrange("p (g d) -> p g d", d=D),
-                prec_sb[:].rearrange("p (g d) -> p g d", d=D),
-                ALU.mult,
-            )
-            nc.vector.tensor_reduce(h[i][:], fit[i][:, :, 0 : D + 1], AX.X, ALU.add)
-            nc.vector.tensor_reduce(low[i][:], h[i][:], AX.X, ALU.min)
+            nc.vector.tensor_reduce(h[i], fit[i][:, :, 0 : D + 1], AX.X, ALU.add)
+            nc.vector.tensor_reduce(low[i][:], h[i], AX.X, ALU.min)
             nc.scalar.activation(
-                ex[i][:], h[i][:], ACT.Exp, bias=low[i][:], scale=-1.0, accum_out=total[i][:]
+                ex[i], h[i], ACT.Exp, bias=low[i][:], scale=-1.0, accum_out=total[:, i : i + 1]
             )
-            nc.vector.tensor_tensor(z[i][:], step[i][:], y[i][:], ALU.add)
 
-        def fuse(i):
-            nc.vector.tensor_tensor(
-                ww[i][:].rearrange("p (g d) -> p g d", d=D),
-                z[i][:].rearrange("p (g d) -> p g d", d=D),
-                ex[i][:].unsqueeze(2).to_broadcast([P, G, D]),
-                ALU.mult,
-            )
-            nc.vector.reciprocal(inv[i][:], total[i][:])
-            for u in range(2):
-                cols = HALF // 16
+        def turn(i):
+            for j in range(2):
+                nc.tensor.transpose(dd_t[i][:, j, :], dd[i][:, j * P : (j + 1) * P], ident[:])
+            for j in range(2):
                 nc.scalar.activation(
-                    wf[i][:, u * HALF : (u + 1) * HALF],
-                    ww[i][:].indirect(byf_sb[:, u * cols : (u + 1) * cols]),
-                    ACT.Copy,
+                    step_t[i][:, j, :], dd_t[i][:, j, :], ACT.Copy, scale=pull[:, j : j + 1]
                 )
 
-        def finish(i):
-            nc.vector.tensor_reduce(
-                fu[i][:], wf[i][:].rearrange("p (v g) -> p v g", g=G), AX.X, ALU.add
-            )
-            nc.scalar.activation(res[i][:], fu[i][:], ACT.Tanh, scale=inv[i][:])
-            nc.sync.dma_start(out[i * P : (i + 1) * P, :], res[i][:])
+        def update(i):
+            step = psum.tile([P, R], F32, name=f"step{i}", tag=f"bank{i}")
+            for j in range(2):
+                nc.tensor.transpose(step[:, j * P : (j + 1) * P], step_t[i][:, j, :], ident[:])
+            nc.vector.tensor_tensor(z[i][:], meas_sb[i], step[:], ALU.add)
 
-        stages = [product, residual, weights, fuse, finish]
-        for turn in range(TILES + len(stages) - 1):
-            for depth, stage in reversed(list(enumerate(stages))):
-                if 0 <= turn - depth < TILES:
-                    stage(turn - depth)
+        def fuse(i):
+            if i in ():
+                for g in range(G):
+                    cols = slice(g * D, (g + 1) * D)
+                    nc.scalar.activation(
+                        ww[i][:, cols], z[i][:, cols], ACT.Copy, scale=ex[i][:, g : g + 1]
+                    )
+            else:
+                nc.vector.tensor_tensor(
+                    ww[i][:, 0:R].rearrange("p (g d) -> p g d", d=D),
+                    grouped(z[i]),
+                    ex[i].unsqueeze(2).to_broadcast([P, G, D]),
+                    ALU.mult,
+                )
+            if i == last:
+                cols = HALF // 16
+                nc.scalar.activation(wf_last[:, 0:HALF], ww[i][:].indirect(byf_sb[:, 0:cols]), ACT.Copy)
+                nc.vector.tensor_copy(wf_last[:, HALF:R], ww[i][:].indirect(byf_sb[:, cols : 2 * cols]))
+            else:
+                nc.scalar.activation(wf[:, i, :], ww[i][:].indirect(byf_sb[:]), ACT.Copy)
+
+        def finish():
+            nc.vector.reciprocal(inv[:], total[:])
+            fu = keep.tile([P, last * D], F32, tag="stats_then_fu")
+            nc.vector.tensor_reduce(
+                fu[:], wf[:].rearrange("p i (v g) -> p (i v) g", g=G), AX.X, ALU.add
+            )
+            nc.vector.tensor_reduce(
+                fu_last[:], wf_last[:].rearrange("p (v g) -> p v g", g=G), AX.X, ALU.add
+            )
+            for i in range(last):
+                nc.scalar.activation(
+                    res[:, i, :], fu[:, i * D : (i + 1) * D], ACT.Tanh, scale=inv[:, i : i + 1]
+                )
+            nc.sync.dma_start(out_rows[:, 0:last, :], res[:])
+            nc.scalar.activation(res_last[:], fu_last[:], ACT.Tanh, scale=inv[:, last:TILES])
+            nc.sync.dma_start(out_rows[:, last, :], res_last[:])
+
+        for i in range(TILES):
+            product(i)
+        for i in range(last):
+            residual(i)
+        misfit(0)
+        residual(last)
+        for i in range(1, TILES):
+            misfit(i)
+        for i in range(TILES):
+            weights(i)
+            turn(i)
+            update(i)
+            fuse(i)
+        finish()

@@ -20,9 +20,13 @@ AX = mybir.AxisListType
 
 P = 128
 PACK = 4
+QUADRANT = 32
+PER_COLUMN = 16
 TILES = S // P
+LAST = TILES - 1
+PAIRS = TILES // 2
+HALVES = R // P
 ROW = D + 4
-HALF = R // 2
 
 
 def tile_picked_yimm_tanh_p_kernel(
@@ -33,42 +37,44 @@ def tile_picked_yimm_tanh_p_kernel(
         keep = ctx.enter_context(tc.tile_pool(name="keep", bufs=1))
         psum = ctx.enter_context(tc.psum_pool(name="psum", bufs=1))
 
-        def tiles(name, shape, dtype, pool=keep, **kw):
-            return [pool.tile(shape, dtype, name=f"{name}{i}", **kw) for i in range(TILES)]
+        def tiles(name, shape, dtype, **kw):
+            return [keep.tile(shape, dtype, name=f"{name}{i}", **kw) for i in range(TILES)]
 
-        offs_sb = keep.tile([P, S // 16], U16)
-        byf_sb = keep.tile([P, R // 16], U16)
+        def by_mode(ap):
+            return ap.rearrange("p (g d) -> p g d", d=D)
+
+        offs_sb = keep.tile([P, S // PER_COLUMN], U16)
+        byf_sb = keep.tile([P, R // PER_COLUMN], U16)
         words_sb = keep.tile([P, T], U32)
         scales_sb = keep.tile([P, T], U8)
         fm_raw = keep.tile([P, PACK, R], F32)
         prec_sb = keep.tile([P, R], F32)
-        gain_col = keep.tile([P, 2], F32)
-        pull = keep.tile([P, 2], F32)
+        gain_col = keep.tile([P, HALVES], F32)
+        gain_less_one = keep.tile([P, HALVES], F32)
         ident = keep.tile([P, P], F32)
         prior_sb = keep.tile([P, G], F32)
-        meas_all = keep.tile([P, TILES, R], F32)
-        meas_sb = [meas_all[:, i, :] for i in range(TILES)]
-        meas_rows = meas.rearrange("(i p) e -> p i e", p=P)
+        meas_sb = keep.tile([P, TILES, R], F32)
 
         nc.gpsimd.memset(scales_sb[:].bitcast(I32), 0)
         nc.sync.dma_start(offs_sb[:], offs)
         nc.sync.dma_start(fm_raw[:], fm.rearrange("(p j) e -> p j e", j=PACK))
-        for q in range(4):
+        for q in range(P // QUADRANT):
             nc.sync.dma_start(
-                scales_sb[32 * q : 32 * q + 4, :].bitcast(I32),
+                scales_sb[QUADRANT * q : QUADRANT * q + 4, :].bitcast(I32),
                 x_scales[0, 4 * q : 4 * q + 4, :].bitcast(I32),
             )
         nc.sync.dma_start(
             words_sb[:].bitcast(I32), x_words[0].rearrange("p c r -> p (c r)").bitcast(I32)
         )
-        nc.sync.dma_start(meas_all[:], meas_rows)
-        nc.sync.dma_start(prec_sb[:], prec)
         nc.sync.dma_start(prior_sb[:], prior)
+        nc.sync.dma_start(meas_sb[:], meas.rearrange("(i p) e -> p i e", p=P))
         with nc.allow_non_contiguous_dma(reason="one gain value to a partition"):
             nc.sync.dma_start(gain_col[:], gain[0:1, :].rearrange("o (j p) -> p (o j)", p=P))
+        nc.sync.dma_start(prec_sb[:], prec)
         nc.sync.dma_start(byf_sb[:], byf)
 
         make_identity(nc, ident[:])
+
         fm_bf = keep.tile([P, R, PACK], BF16, align_bytes=64)
         fm_codes = keep.tile([P, R], U32, align_bytes=64)
         fm_scales = keep.tile([P, R], U8, align_bytes=64)
@@ -77,137 +83,134 @@ def tile_picked_yimm_tanh_p_kernel(
             fm_raw[:].rearrange("p j (c i) -> p c j i", i=4),
             ACT.Copy,
         )
-        x_sc = keep.tile([P, S], U8, align_bytes=64)
-        nc.vector.tensor_copy(x_sc[:], scales_sb[:].indirect(offs_sb[:]))
+        picked_scales = keep.tile([P, S], U8, align_bytes=64)
+        nc.vector.tensor_copy(picked_scales[:], scales_sb[:].indirect(offs_sb[:]))
         nc.vector.quantize_mx(
             out=fm_codes[:].bitcast(FP8X4),
             scales=fm_scales[:],
             in_=fm_bf[:].rearrange("p e j -> p (e j)"),
         )
 
-        x_codes = tiles("x_codes", [P, P], U32, align_bytes=64)
+        picked_words = tiles("picked_words", [P, P], U32, align_bytes=64)
         y = [psum.tile([P, R], F32, name=f"y{i}", tag=f"bank{i}") for i in range(TILES)]
         dd = tiles("dd", [P, R], F32)
-        sq = tiles("sq", [P, R], F32)
-        fit = tiles("fit", [P, G, ROW], F32)
-        dd_t = tiles("dd_t", [P, 2, P], F32, pool=psum)
-        step_t = tiles("step_t", [P, 2, P], F32)
-        z = tiles("z", [P, R], F32)
-        last = TILES - 1
-        ww = [keep.tile([P, R + 2 * G if i < last else R], F32, name=f"ww{i}") for i in range(TILES)]
-        wf = keep.tile([P, last, R], F32)
-        wf_last = keep.tile([P, R], F32)
-        stats_last = keep.tile([P, last * D], F32, tag="stats_then_fu")
-        h = [ww[i][:, R : R + G] for i in range(last)] + [stats_last[:, 0:G]]
+        half_sq = tiles("half_sq", [P, R], F32)
+        terms = tiles("terms", [P, G, ROW], F32)
+        dd_t = [psum.tile([P, HALVES, 2, P], F32, name=f"dd_t{a}") for a in range(PAIRS)]
+        pull_t = [keep.tile([P, HALVES, 2, P], F32, name=f"pull_t{a}") for a in range(PAIRS)]
+        z = [keep.tile([P, R], F32, name=f"z{i}", tag=f"z{i}") for i in range(TILES)]
+        ww = [keep.tile([P, R + G], F32, name=f"ww{i}") for i in range(LAST)]
+        ww.append(keep.tile([P, R + TILES], F32, name="ww_last"))
+        ex_first = keep.tile([P, G], F32)
+        ex = [ex_first[:]] + [ww[i][:, R : R + G] for i in range(LAST)]
+        total = ww[LAST][:, R : R + TILES]
+        inv_total = keep.tile([P, TILES], F32)
+        neg_lm_early = keep.tile([P, LAST, G], F32)
         low = tiles("low", [P, 1], F32)
-        ex = [ww[i][:, R + G : R + 2 * G] for i in range(last)] + [stats_last[:, G : 2 * G]]
-        total = keep.tile([P, TILES], F32)
-        inv = keep.tile([P, TILES], F32)
+        wf_early = keep.tile([P, LAST, R], F32)
+        wf_last = keep.tile([P, R], F32)
+        wf = [wf_early[:, i, :] for i in range(LAST)] + [wf_last[:]]
         fu_last = keep.tile([P, D], F32)
-        res = keep.tile([P, last, D], F32)
+        res_early = keep.tile([P, LAST, D], F32)
         res_last = keep.tile([P, D], F32)
         out_rows = out.rearrange("(i p) v -> p i v", p=P)
 
         for i in range(TILES):
-            nc.scalar.activation(fit[i][:, :, D], prior_sb[:], ACT.Copy, scale=-1.0)
-        nc.scalar.activation(pull[:], gain_col[:], ACT.Copy, bias=-1.0)
+            nc.scalar.activation(terms[i][:, :, D], prior_sb[:], ACT.Copy, scale=-1.0)
+        nc.gpsimd.tensor_scalar(gain_less_one[:], gain_col[:], 1.0, -1.0, ALU.mult, ALU.add)
 
         def product(i):
-            cols = P // 16
+            cols = P // PER_COLUMN
             nc.vector.tensor_copy(
-                x_codes[i][:], words_sb[:].indirect(offs_sb[:, i * cols : (i + 1) * cols])
+                picked_words[i][:], words_sb[:].indirect(offs_sb[:, i * cols : (i + 1) * cols])
             )
             nc.tensor.matmul_mx(
                 out=y[i][:],
-                lhsT=x_codes[i][:].bitcast(FP8X4),
-                lhsT_scale=x_sc[:, i * P : (i + 1) * P],
+                lhsT=picked_words[i][:].bitcast(FP8X4),
+                lhsT_scale=picked_scales[:, i * P : (i + 1) * P],
                 rhs=fm_codes[:].bitcast(FP8X4),
                 rhs_scale=fm_scales[:],
                 start=True,
                 stop=True,
             )
 
-        def grouped(tile):
-            return tile[:].rearrange("p (g d) -> p g d", d=D)
-
         def residual(i):
-            nc.vector.tensor_tensor(dd[i][:], meas_sb[i], y[i][:], ALU.subtract)
-            nc.scalar.activation(sq[i][:], dd[i][:], ACT.Square, scale=math.sqrt(0.5))
+            nc.vector.tensor_tensor(dd[i][:], meas_sb[:, i, :], y[i][:], ALU.subtract)
+            nc.scalar.activation(half_sq[i][:], dd[i][:], ACT.Square, scale=math.sqrt(0.5))
 
         def misfit(i):
-            weng = nc.gpsimd if i in (1, 2, 3) else nc.vector
-            weng.tensor_tensor(fit[i][:, :, 0:D], grouped(sq[i]), grouped(prec_sb), ALU.mult)
-
-        def weights(i):
-            nc.vector.tensor_reduce(h[i], fit[i][:, :, 0 : D + 1], AX.X, ALU.add)
-            nc.vector.tensor_reduce(low[i][:], h[i], AX.X, ALU.min)
-            nc.scalar.activation(
-                ex[i], h[i], ACT.Exp, bias=low[i][:], scale=-1.0, accum_out=total[:, i : i + 1]
+            engine = nc.vector if i == 0 else nc.gpsimd
+            engine.tensor_tensor(
+                terms[i][:, :, 0:D], by_mode(half_sq[i][:]), by_mode(prec_sb[:]), ALU.mult
             )
 
-        def turn(i):
-            for j in range(2):
-                nc.tensor.transpose(dd_t[i][:, j, :], dd[i][:, j * P : (j + 1) * P], ident[:])
-            for j in range(2):
-                nc.scalar.activation(
-                    step_t[i][:, j, :], dd_t[i][:, j, :], ACT.Copy, scale=pull[:, j : j + 1]
-                )
+        def weights(i, neg_lm):
+            nc.vector.tensor_reduce(neg_lm, terms[i][:, :, 0 : D + 1], AX.X, ALU.add)
+            nc.vector.tensor_reduce(low[i][:], neg_lm, AX.X, ALU.min)
+            nc.scalar.activation(
+                ex[i], neg_lm, ACT.Exp, bias=low[i][:], scale=-1.0, accum_out=total[:, i : i + 1]
+            )
 
-        def update(i):
-            step = psum.tile([P, R], F32, name=f"step{i}", tag=f"bank{i}")
-            for j in range(2):
-                nc.tensor.transpose(step[:, j * P : (j + 1) * P], step_t[i][:, j, :], ident[:])
-            nc.vector.tensor_tensor(z[i][:], meas_sb[i], step[:], ALU.add)
+        def pull(a):
+            for b in range(2):
+                for j in range(HALVES):
+                    nc.tensor.transpose(
+                        dd_t[a][:, j, b, :], dd[2 * a + b][:, j * P : (j + 1) * P], ident[:]
+                    )
+            for j in range(HALVES):
+                nc.scalar.activation(
+                    pull_t[a][:, j], dd_t[a][:, j], ACT.Copy, scale=gain_less_one[:, j : j + 1]
+                )
 
         def fuse(i):
-            if i in ():
-                for g in range(G):
-                    cols = slice(g * D, (g + 1) * D)
-                    nc.scalar.activation(
-                        ww[i][:, cols], z[i][:, cols], ACT.Copy, scale=ex[i][:, g : g + 1]
-                    )
-            else:
-                nc.vector.tensor_tensor(
-                    ww[i][:, 0:R].rearrange("p (g d) -> p g d", d=D),
-                    grouped(z[i]),
-                    ex[i].unsqueeze(2).to_broadcast([P, G, D]),
-                    ALU.mult,
+            pull_back = psum.tile([P, R], F32, name=f"pull_back{i}", tag=f"bank{i}")
+            for j in range(HALVES):
+                nc.tensor.transpose(
+                    pull_back[:, j * P : (j + 1) * P], pull_t[i // 2][:, j, i % 2, :], ident[:]
                 )
-            if i == last:
-                cols = HALF // 16
-                nc.scalar.activation(wf_last[:, 0:HALF], ww[i][:].indirect(byf_sb[:, 0:cols]), ACT.Copy)
-                nc.vector.tensor_copy(wf_last[:, HALF:R], ww[i][:].indirect(byf_sb[:, cols : 2 * cols]))
-            else:
-                nc.scalar.activation(wf[:, i, :], ww[i][:].indirect(byf_sb[:]), ACT.Copy)
-
-        def finish():
-            nc.vector.reciprocal(inv[:], total[:])
-            fu = keep.tile([P, last * D], F32, tag="stats_then_fu")
-            nc.vector.tensor_reduce(
-                fu[:], wf[:].rearrange("p i (v g) -> p (i v) g", g=G), AX.X, ALU.add
+            nc.vector.tensor_tensor(z[i][:], meas_sb[:, i, :], pull_back[:], ALU.add)
+            nc.vector.tensor_tensor(
+                by_mode(ww[i][:, 0:R]),
+                by_mode(z[i][:]),
+                ex[i].unsqueeze(2).to_broadcast([P, G, D]),
+                ALU.mult,
             )
-            nc.vector.tensor_reduce(
-                fu_last[:], wf_last[:].rearrange("p (v g) -> p v g", g=G), AX.X, ALU.add
-            )
-            for i in range(last):
-                nc.scalar.activation(
-                    res[:, i, :], fu[:, i * D : (i + 1) * D], ACT.Tanh, scale=inv[:, i : i + 1]
-                )
-            nc.sync.dma_start(out_rows[:, 0:last, :], res[:])
-            nc.scalar.activation(res_last[:], fu_last[:], ACT.Tanh, scale=inv[:, last:TILES])
-            nc.sync.dma_start(out_rows[:, last, :], res_last[:])
+            nc.scalar.activation(wf[i], ww[i][:].indirect(byf_sb[:]), ACT.Copy)
 
         for i in range(TILES):
             product(i)
-        for i in range(last):
+        for i in range(LAST):
             residual(i)
         misfit(0)
-        residual(last)
+        residual(LAST)
         for i in range(1, TILES):
             misfit(i)
-        for i in range(TILES):
-            weights(i)
-            turn(i)
-            update(i)
-            fuse(i)
-        finish()
+        for i in range(LAST):
+            weights(i, neg_lm_early[:, i, :])
+        for a in range(PAIRS):
+            pull(a)
+        fuse(0)
+        fuse(1)
+        neg_lm_last = keep.tile([P, G], F32, tag="z1")
+        weights(LAST, neg_lm_last[:])
+        fuse(2)
+        fuse(LAST)
+
+        nc.vector.reciprocal(inv_total[:], total)
+        fu_early = keep.tile([P, LAST * D], F32, tag=f"z{LAST}")
+        nc.vector.tensor_reduce(
+            fu_early[:], wf_early[:].rearrange("p i (v g) -> p (i v) g", g=G), AX.X, ALU.add
+        )
+        nc.vector.tensor_reduce(
+            fu_last[:], wf_last[:].rearrange("p (v g) -> p v g", g=G), AX.X, ALU.add
+        )
+        for i in range(LAST):
+            nc.scalar.activation(
+                res_early[:, i, :],
+                fu_early[:, i * D : (i + 1) * D],
+                ACT.Tanh,
+                scale=inv_total[:, i : i + 1],
+            )
+        nc.sync.dma_start(out_rows[:, 0:LAST, :], res_early[:])
+        nc.scalar.activation(res_last[:], fu_last[:], ACT.Tanh, scale=inv_total[:, LAST:TILES])
+        nc.sync.dma_start(out_rows[:, LAST, :], res_last[:])

import math
from contextlib import ExitStack

import concourse.mybir as mybir
from concourse.masks import make_identity

K, T, S, D, R, G = 512, 2048, 512, 32, 256, 8
FLOPS = 2 * K * S * R

F32 = mybir.dt.float32
BF16 = mybir.dt.bfloat16
I32 = mybir.dt.int32
U32 = mybir.dt.uint32
U16 = mybir.dt.uint16
U8 = mybir.dt.uint8
FP8X4 = mybir.dt.float8_e4m3fn_x4
ALU = mybir.AluOpType
ACT = mybir.ActivationFunctionType
AX = mybir.AxisListType

P = 128
PACK = 4
QUADRANT = 32
PER_COLUMN = 16
TILES = S // P
LAST = TILES - 1
PAIRS = TILES // 2
HALVES = R // P
ROW = D + 4


def tile_picked_yimm_tanh_p_kernel(
    tc, x_words, x_scales, fm, meas, prec, prior, gain, offs, byf, out
):
    nc = tc.nc
    with ExitStack() as ctx:
        keep = ctx.enter_context(tc.tile_pool(name="keep", bufs=1))
        psum = ctx.enter_context(tc.psum_pool(name="psum", bufs=1))

        def tiles(name, shape, dtype, **kw):
            return [keep.tile(shape, dtype, name=f"{name}{i}", **kw) for i in range(TILES)]

        def by_mode(ap):
            return ap.rearrange("p (g d) -> p g d", d=D)

        offs_sb = keep.tile([P, S // PER_COLUMN], U16)
        byf_sb = keep.tile([P, R // PER_COLUMN], U16)
        words_sb = keep.tile([P, T], U32)
        scales_sb = keep.tile([P, T], U8)
        fm_raw = keep.tile([P, PACK, R], F32)
        prec_sb = keep.tile([P, R], F32)
        gain_col = keep.tile([P, HALVES], F32)
        gain_less_one = keep.tile([P, HALVES], F32)
        ident = keep.tile([P, P], F32)
        prior_sb = keep.tile([P, G], F32)
        meas_sb = keep.tile([P, TILES, R], F32)

        nc.gpsimd.memset(scales_sb[:].bitcast(I32), 0)
        nc.sync.dma_start(offs_sb[:], offs)
        nc.sync.dma_start(fm_raw[:], fm.rearrange("(p j) e -> p j e", j=PACK))
        for q in range(P // QUADRANT):
            nc.sync.dma_start(
                scales_sb[QUADRANT * q : QUADRANT * q + 4, :].bitcast(I32),
                x_scales[0, 4 * q : 4 * q + 4, :].bitcast(I32),
            )
        nc.sync.dma_start(
            words_sb[:].bitcast(I32), x_words[0].rearrange("p c r -> p (c r)").bitcast(I32)
        )
        nc.sync.dma_start(prior_sb[:], prior)
        nc.sync.dma_start(meas_sb[:], meas.rearrange("(i p) e -> p i e", p=P))
        with nc.allow_non_contiguous_dma(reason="one gain value to a partition"):
            nc.sync.dma_start(gain_col[:], gain[0:1, :].rearrange("o (j p) -> p (o j)", p=P))
        nc.sync.dma_start(prec_sb[:], prec)
        nc.sync.dma_start(byf_sb[:], byf)

        make_identity(nc, ident[:])

        fm_bf = keep.tile([P, R, PACK], BF16, align_bytes=64)
        fm_codes = keep.tile([P, R], U32, align_bytes=64)
        fm_scales = keep.tile([P, R], U8, align_bytes=64)
        nc.scalar.activation(
            fm_bf[:].rearrange("p (c i) j -> p c j i", i=4),
            fm_raw[:].rearrange("p j (c i) -> p c j i", i=4),
            ACT.Copy,
        )
        picked_scales = keep.tile([P, S], U8, align_bytes=64)
        nc.vector.tensor_copy(picked_scales[:], scales_sb[:].indirect(offs_sb[:]))
        nc.vector.quantize_mx(
            out=fm_codes[:].bitcast(FP8X4),
            scales=fm_scales[:],
            in_=fm_bf[:].rearrange("p e j -> p (e j)"),
        )

        picked_words = tiles("picked_words", [P, P], U32, align_bytes=64)
        y = [psum.tile([P, R], F32, name=f"y{i}", tag=f"bank{i}") for i in range(TILES)]
        dd = tiles("dd", [P, R], F32)
        half_sq = tiles("half_sq", [P, R], F32)
        terms = tiles("terms", [P, G, ROW], F32)
        dd_t = [psum.tile([P, HALVES, 2, P], F32, name=f"dd_t{a}") for a in range(PAIRS)]
        pull_t = [keep.tile([P, HALVES, 2, P], F32, name=f"pull_t{a}") for a in range(PAIRS)]
        z = [keep.tile([P, R], F32, name=f"z{i}", tag=f"z{i}") for i in range(TILES)]
        ww = [keep.tile([P, R + G], F32, name=f"ww{i}") for i in range(LAST)]
        ww.append(keep.tile([P, R + TILES], F32, name="ww_last"))
        ex_first = keep.tile([P, G], F32)
        ex = [ex_first[:]] + [ww[i][:, R : R + G] for i in range(LAST)]
        total = ww[LAST][:, R : R + TILES]
        inv_total = keep.tile([P, TILES], F32)
        neg_lm_early = keep.tile([P, LAST, G], F32)
        low = tiles("low", [P, 1], F32)
        wf_early = keep.tile([P, LAST, R], F32)
        wf_last = keep.tile([P, R], F32)
        wf = [wf_early[:, i, :] for i in range(LAST)] + [wf_last[:]]
        fu_last = keep.tile([P, D], F32)
        res_early = keep.tile([P, LAST, D], F32)
        res_last = keep.tile([P, D], F32)
        out_rows = out.rearrange("(i p) v -> p i v", p=P)

        for i in range(TILES):
            nc.scalar.activation(terms[i][:, :, D], prior_sb[:], ACT.Copy, scale=-1.0)
        nc.gpsimd.tensor_scalar(gain_less_one[:], gain_col[:], 1.0, -1.0, ALU.mult, ALU.add)

        def product(i):
            cols = P // PER_COLUMN
            nc.vector.tensor_copy(
                picked_words[i][:], words_sb[:].indirect(offs_sb[:, i * cols : (i + 1) * cols])
            )
            nc.tensor.matmul_mx(
                out=y[i][:],
                lhsT=picked_words[i][:].bitcast(FP8X4),
                lhsT_scale=picked_scales[:, i * P : (i + 1) * P],
                rhs=fm_codes[:].bitcast(FP8X4),
                rhs_scale=fm_scales[:],
                start=True,
                stop=True,
            )

        def residual(i):
            nc.vector.tensor_tensor(dd[i][:], meas_sb[:, i, :], y[i][:], ALU.subtract)
            nc.scalar.activation(half_sq[i][:], dd[i][:], ACT.Square, scale=math.sqrt(0.5))

        def misfit(i):
            engine = nc.vector if i == 0 else nc.gpsimd
            engine.tensor_tensor(
                terms[i][:, :, 0:D], by_mode(half_sq[i][:]), by_mode(prec_sb[:]), ALU.mult
            )

        def weights(i, neg_lm):
            nc.vector.tensor_reduce(neg_lm, terms[i][:, :, 0 : D + 1], AX.X, ALU.add)
            nc.vector.tensor_reduce(low[i][:], neg_lm, AX.X, ALU.min)
            nc.scalar.activation(
                ex[i], neg_lm, ACT.Exp, bias=low[i][:], scale=-1.0, accum_out=total[:, i : i + 1]
            )

        def pull(a):
            for b in range(2):
                for j in range(HALVES):
                    nc.tensor.transpose(
                        dd_t[a][:, j, b, :], dd[2 * a + b][:, j * P : (j + 1) * P], ident[:]
                    )
            for j in range(HALVES):
                nc.scalar.activation(
                    pull_t[a][:, j], dd_t[a][:, j], ACT.Copy, scale=gain_less_one[:, j : j + 1]
                )

        def fuse(i):
            pull_back = psum.tile([P, R], F32, name=f"pull_back{i}", tag=f"bank{i}")
            for j in range(HALVES):
                nc.tensor.transpose(
                    pull_back[:, j * P : (j + 1) * P], pull_t[i // 2][:, j, i % 2, :], ident[:]
                )
            nc.vector.tensor_tensor(z[i][:], meas_sb[:, i, :], pull_back[:], ALU.add)
            nc.vector.tensor_tensor(
                by_mode(ww[i][:, 0:R]),
                by_mode(z[i][:]),
                ex[i].unsqueeze(2).to_broadcast([P, G, D]),
                ALU.mult,
            )
            nc.scalar.activation(wf[i], ww[i][:].indirect(byf_sb[:]), ACT.Copy)

        for i in range(TILES):
            product(i)
        for i in range(LAST):
            residual(i)
        misfit(0)
        residual(LAST)
        for i in range(1, TILES):
            misfit(i)
        for i in range(LAST):
            weights(i, neg_lm_early[:, i, :])
        for a in range(PAIRS):
            pull(a)
        fuse(0)
        fuse(1)
        neg_lm_last = keep.tile([P, G], F32, tag="z1")
        weights(LAST, neg_lm_last[:])
        fuse(2)
        fuse(LAST)

        nc.vector.reciprocal(inv_total[:], total)
        fu_early = keep.tile([P, LAST * D], F32, tag=f"z{LAST}")
        nc.vector.tensor_reduce(
            fu_early[:], wf_early[:].rearrange("p i (v g) -> p (i v) g", g=G), AX.X, ALU.add
        )
        nc.vector.tensor_reduce(
            fu_last[:], wf_last[:].rearrange("p (v g) -> p v g", g=G), AX.X, ALU.add
        )
        for i in range(LAST):
            nc.scalar.activation(
                res_early[:, i, :],
                fu_early[:, i * D : (i + 1) * D],
                ACT.Tanh,
                scale=inv_total[:, i : i + 1],
            )
        nc.sync.dma_start(out_rows[:, 0:LAST, :], res_early[:])
        nc.scalar.activation(res_last[:], fu_last[:], ACT.Tanh, scale=inv_total[:, LAST:TILES])
        nc.sync.dma_start(out_rows[:, LAST, :], res_last[:])
